import numpy as np
import ml_dtypes


def mxq(x, axis, fmt="e4m3"):
    dtype, down = {"e4m3": (ml_dtypes.float8_e4m3fn, 7), "e5m2": (ml_dtypes.float8_e5m2, 14)}[fmt]
    v = np.moveaxis(np.asarray(x, np.float32).astype(ml_dtypes.bfloat16).astype(np.float64), axis, -1)
    blocks = v.reshape(v.shape[:-1] + (-1, 32))
    amax = np.abs(blocks).max(-1, keepdims=True)
    byte = np.maximum(np.where(amax > 0, np.frexp(amax)[1] - 1 + 127, 0) - down, 1)
    scale = np.exp2(byte - 127.0)
    codes = (blocks / scale).astype(np.float32).astype(dtype).astype(np.float64)
    return np.moveaxis((codes * scale).reshape(v.shape), -1, axis)


WIDE = False


def mx_kscale(k):
    if not WIDE:
        return np.ones(k)
    levels = np.array([24, -24, 12, -12, 0])
    if k % 512:
        return np.exp2(np.random.permutation(np.resize(levels, k // 32))).repeat(32)
    a = np.empty((k // 512, 16))
    for p in range(k // 512):
        a[p, :8] = np.random.permutation(np.resize(levels, 8))
        for g in range(8):
            far = levels[np.abs(levels - a[p, g]) >= 10]
            a[p, g + 8] = far[np.random.randint(len(far))]
    return np.exp2(a.ravel()).repeat(32)


def f64(x):
    return np.asarray(x).astype(np.float64)


def striped8(idx):
    return np.concatenate([v.reshape(-1, 16).T for v in idx]).astype(np.uint16)


def unstriped8(offs):
    return np.stack([offs[16 * g:16 * g + 16].T.reshape(-1) for g in range(8)]).astype(np.int64)


def silu(f):
    return f / (1.0 + np.exp(-np.maximum(f, -700.0)))


K, N, T, J = 1024, 512, 2048, 1024


def setup_inputs():
    n = np.random.standard_normal
    s = mx_kscale(K)[:, None]
    return {
        "xT": (n((K, T)) * s).astype(np.float32),
        "wgt": np.repeat(np.random.uniform(0.5, 2.0, (8, J)), 16, axis=0).astype(np.float32),
        "wk": (n((K, N)) / np.sqrt(K) / s).astype(np.float32),
        "wv": (n((K, N)) / np.sqrt(K) / s).astype(np.float32),
        "st": (n((N, J))).astype(np.float32),
        "offs": striped8(np.stack([np.random.permutation(T)[:J] for _ in range(8)])),
    }


def reference(xT, wgt, wk, wv, st, offs):
    idx = unstriped8(offs)
    rows = np.arange(K)
    xg = f64(wgt)[rows // 4 % 128] * f64(xT)[rows[:, None], idx[rows % 512 // 64]]
    xT_ = mxq(xg, 0, "e4m3")
    wk_ = mxq(f64(wk), 0, "e4m3")
    wv_ = mxq(f64(wv), 0, "e4m3")
    ke = wk_.T @ xT_
    ve = wv_.T @ xT_
    gate = silu(ke * f64(st))
    return gate * ve

@@ -1,0 +1,190 @@
+from contextlib import ExitStack
+
+import concourse.mybir as mybir
+
+K, N, T, J = 1024, 512, 2048, 1024
+FLOPS = 2 * 2 * K * N * J
+
+F32 = mybir.dt.float32
+BF16 = mybir.dt.bfloat16
+U32 = mybir.dt.uint32
+U16 = mybir.dt.uint16
+U8 = mybir.dt.uint8
+FP8X4 = mybir.dt.float8_e4m3fn_x4
+MULT = mybir.AluOpType.mult
+ADD = mybir.AluOpType.add
+SILU = mybir.ActivationFunctionType.Silu
+
+P = 128
+PACK = 4
+K_PASS = P * PACK
+PASSES = K // K_PASS
+HALF = 512
+HALVES = J // HALF
+N_TILES = N // P
+CHUNKS = [[512,512],[256,256,512]]
+WCOLS = 256
+
+
+def tile_list_silu_kernel(tc, xT, wgt, wk, wv, st, offs, out):
+    nc = tc.nc
+    with ExitStack() as ctx:
+        keep = ctx.enter_context(tc.tile_pool(name="keep", bufs=1))
+        ring = ctx.enter_context(tc.tile_pool(name="ring", bufs=3))
+        psum = ctx.enter_context(tc.psum_pool(name="psum", bufs=1))
+
+        offsets = keep.tile([P, J // 16], U16, name="offsets")
+        nc.sync.dma_start(offsets[:], offs)
+
+        x_rows = xT.rearrange("(a p i) t -> a i p t", a=PASSES, i=PACK)
+        planes, w_raw, st_sb, wgt_sb = {}, {}, {}, {}
+        picked, x_codes, x_scales, w_codes, w_scales = {}, {}, {}, {}, {}
+        ke, ve, gate, xg, wg = {}, {}, {}, {}, {}
+
+        def interleave(eng, grouped, rows):
+            dst = grouped.rearrange("p (c i) t -> p c t i", i=4)
+            src = rows.rearrange("p t (c i) -> p c t i", i=4)
+            if eng == "S":
+                nc.scalar.copy(dst, src)
+            elif eng == "V":
+                nc.vector.tensor_copy(dst, src)
+            else:
+                nc.gpsimd.tensor_scalar(dst, src, 1.0, 0.0, MULT, ADD)
+
+        def quantize(codes, scales, grouped):
+            nc.vector.quantize_mx(out=codes.bitcast(FP8X4), scales=scales, in_=grouped.rearrange("p w t -> p (w t)"))
+
+        def LX(a, i):
+            planes[a, i] = keep.tile([P, T], F32, name="plane_%d_%d" % (a, i))
+            nc.sync.dma_start(planes[a, i][:], x_rows[a, i])
+
+        def LG(c0, c1):
+            wgt_sb[c0] = keep.tile([P, c1 - c0], F32, name="wgt_%d" % c0)
+            nc.sync.dma_start(wgt_sb[c0][:], wgt[:, c0:c1])
+
+        def wgt_cols(c0, c1):
+            base = max(b for b in wgt_sb if b <= c0)
+            return wgt_sb[base][:, c0 - base : c1 - base]
+
+        def LW(m, a, c):
+            w = (wk, wv)[m]
+            w_raw[m, a, c] = keep.tile([P, PACK, WCOLS], F32, name="w_raw_%d_%d_%d" % (m, a, c))
+            rows = w[a * K_PASS : (a + 1) * K_PASS, c * WCOLS : (c + 1) * WCOLS]
+            nc.sync.dma_start(w_raw[m, a, c][:], rows.rearrange("(p i) n -> p i n", i=PACK))
+
+        def LS(n, h):
+            st_sb[n, h] = keep.tile([P, HALF], F32, name="st_%d_%d" % (n, h))
+            nc.sync.dma_start(st_sb[n, h][:], st[n * P : (n + 1) * P, h * HALF : (h + 1) * HALF])
+
+        def span(a, c):
+            c0 = sum(CHUNKS[a][:c])
+            return c0, c0 + CHUNKS[a][c]
+
+        def G(a, i, c):
+            c0, c1 = span(a, c)
+            if (a, c) not in picked:
+                picked[a, c] = keep.tile([P, PACK, c1 - c0], F32, name="picked_%d_%d" % (a, c))
+            nc.vector.tensor_tensor(
+                picked[a, c][:, i, :], planes[a, i][:].indirect(offsets[:, c0 // 16 : c1 // 16]), wgt_cols(c0, c1), MULT
+            )
+
+        def IX(a, c, eng):
+            c0, c1 = span(a, c)
+            xg[a, c] = ring.tile([P, c1 - c0, PACK], BF16, name="x_grouped", align_bytes=64, bufs=4)
+            interleave(eng, xg[a, c][:], picked[a, c][:])
+
+        def QX(a, c):
+            c0, c1 = span(a, c)
+            h = c0 // HALF
+            if (a, h) not in x_codes:
+                x_codes[a, h] = keep.tile([P, HALF], U32, name="x_codes_%d_%d" % (a, h), align_bytes=64)
+                x_scales[a, h] = keep.tile([P, HALF], U8, name="x_scales_%d_%d" % (a, h), align_bytes=64)
+            cols = slice(c0 - h * HALF, c1 - h * HALF)
+            quantize(x_codes[a, h][:, cols], x_scales[a, h][:, cols], xg[a, c][:])
+
+        def IW(m, a, c, eng):
+            wg[m, a, c] = ring.tile([P, WCOLS, PACK], BF16, name="w_grouped", align_bytes=64, bufs=4)
+            interleave(eng, wg[m, a, c][:], w_raw[m, a, c][:])
+
+        def QW(m, a, c):
+            w_codes[m, a, c] = keep.tile([P, WCOLS], U32, name="w_codes_%d_%d_%d" % (m, a, c), align_bytes=64)
+            w_scales[m, a, c] = keep.tile([P, WCOLS], U8, name="w_scales_%d_%d_%d" % (m, a, c), align_bytes=64)
+            quantize(w_codes[m, a, c][:], w_scales[m, a, c][:], wg[m, a, c][:])
+
+        def MM(m, a, n, h):
+            banks = (ke, ve)[m]
+            if a == 0:
+                banks[n, h] = psum.tile([P, HALF], F32, name=("ke", "ve")[m], tag="bank_%d" % BANK(m, n, h))
+            c, r = divmod(n * P, WCOLS)
+            cols = slice(r, r + P)
+            nc.tensor.matmul_mx(
+                out=banks[n, h][:],
+                lhsT=w_codes[m, a, c][:, cols].bitcast(FP8X4),
+                lhsT_scale=w_scales[m, a, c][:, cols],
+                rhs=x_codes[a, h][:].bitcast(FP8X4),
+                rhs_scale=x_scales[a, h][:],
+                start=(a == 0),
+                stop=(a == PASSES - 1),
+            )
+
+        def A(n, h):
+            f = ring.tile([P, HALF], F32, name="f", bufs=4)
+            nc.vector.tensor_tensor(f[:], ke[n, h][:], st_sb[n, h][:], MULT)
+            gate[n, h] = keep.tile([P, HALF], F32, name="gate_%d_%d" % (n, h))
+            nc.scalar.activation(gate[n, h][:], f[:], SILU)
+
+        def C(n, h, eng="V"):
+            res = keep.tile([P, HALF], F32, name="res", tag="st_%d_%d" % (n, h))
+            if eng == "V":
+                nc.vector.tensor_tensor(res[:], ve[n, h][:], gate[n, h][:], MULT)
+            else:
+                vs = ring.tile([P, HALF], F32, name="ve_sb", bufs=2)
+                nc.scalar.copy(vs[:], ve[n, h][:])
+                nc.gpsimd.tensor_tensor(res[:], vs[:], gate[n, h][:], MULT)
+            nc.sync.dma_start(out[n * P : (n + 1) * P, h * HALF : (h + 1) * HALF], res[:])
+
+        def BANK(m, n, h):
+            return 2 * n + h
+
+        warm = keep.tile([P, 8], F32, name="warm")
+        nc.vector.memset(warm[:], 0.0)
+        nc.scalar.activation(warm[:, 0:1], warm[:, 1:2], SILU)
+
+        LX(0, 0); LG(0, 512); LG(512, 1024); LX(0, 1); LX(0, 2); LX(0, 3); LX(1, 0); LW(0, 0, 0); LW(0, 0, 1); LX(1, 1); LW(0, 1, 0); LX(1, 2); LW(0, 1, 1); LX(1, 3); LW(1, 0, 0); LW(1, 1, 0)
+        for n in range(4):
+            LS(n, 0)
+        LW(1, 0, 1); LW(1, 1, 1)
+        for n in range(4):
+            LS(n, 1)
+        E1, E2, E3 = "VSS"
+        for i in range(4):
+            for c in range(len(CHUNKS[0])):
+                G(0, i, c)
+        for c in range(len(CHUNKS[0])):
+            IX(0, c, "S"); QX(0, c)
+        for a in range(2):
+            for c in range(2):
+                IW(0, a, c, "S"); QW(0, a, c)
+        for h in range(2):
+            for n in range(4):
+                MM(0, 0, n, h)
+        IW(1, 0, 0, "S"); QW(1, 0, 0)
+        for i in range(4):
+            for c in range(len(CHUNKS[1])):
+                G(1, i, c)
+        for c in range(len(CHUNKS[1])):
+            IX(1, c, "S"); QX(1, c)
+        for h in range(2):
+            for n in range(4):
+                MM(0, 1, n, h)
+        IW(1, 1, 0, E1); QW(1, 1, 0)
+        for n in range(4):
+            A(n, 0)
+        for n in range(2):
+            MM(1, 0, n, 0); MM(1, 1, n, 0); C(n, 0)
+        IW(1, 0, 1, E2); QW(1, 0, 1)
+        IW(1, 1, 1, E3); QW(1, 1, 1)
+        for n in range(4):
+            A(n, 1)
+        for n, h in ((0, 1), (1, 1), (2, 0), (3, 0), (2, 1), (3, 1)):
+            MM(1, 0, n, h); MM(1, 1, n, h); C(n, h)

@@ -22,8 +22,10 @@ PASSES = K // K_PASS
 HALF = 512
 HALVES = J // HALF
 N_TILES = N // P
-CHUNKS = [[512,512],[256,256,512]]
+CHUNKS = [[512,512],[256,256,256,256]]
 WCOLS = 256
+XT = {}
+WT = {0: "plane_1_2"}
 
 
 def tile_list_silu_kernel(tc, xT, wgt, wk, wv, st, offs, out):
@@ -34,12 +36,11 @@ def tile_list_silu_kernel(tc, xT, wgt, wk, wv, st, offs, out):
         psum = ctx.enter_context(tc.psum_pool(name="psum", bufs=1))
 
         offsets = keep.tile([P, J // 16], U16, name="offsets")
-        nc.sync.dma_start(offsets[:], offs)
 
         x_rows = xT.rearrange("(a p i) t -> a i p t", a=PASSES, i=PACK)
         planes, w_raw, st_sb, wgt_sb = {}, {}, {}, {}
         picked, x_codes, x_scales, w_codes, w_scales = {}, {}, {}, {}, {}
-        ke, ve, gate, xg, wg = {}, {}, {}, {}, {}
+        ke, ve, gate, xg, wg, res = {}, {}, {}, {}, {}, {}
 
         def interleave(eng, grouped, rows):
             dst = grouped.rearrange("p (c i) t -> p c t i", i=4)
@@ -55,72 +56,82 @@ def tile_list_silu_kernel(tc, xT, wgt, wk, wv, st, offs, out):
             nc.vector.quantize_mx(out=codes.bitcast(FP8X4), scales=scales, in_=grouped.rearrange("p w t -> p (w t)"))
 
         def LX(a, i):
-            planes[a, i] = keep.tile([P, T], F32, name="plane_%d_%d" % (a, i))
+            planes[a, i] = keep.tile([P, T], F32, name="plane_%d_%d" % (a, i), align_bytes=64)
             nc.sync.dma_start(planes[a, i][:], x_rows[a, i])
 
-        def LG(c0, c1):
-            wgt_sb[c0] = keep.tile([P, c1 - c0], F32, name="wgt_%d" % c0)
-            nc.sync.dma_start(wgt_sb[c0][:], wgt[:, c0:c1])
+        def LG():
+            compact = keep.tile([P, 2, 32], F32, name="wgt_compact", align_bytes=64)
+            for q in range(4):
+                rows = wgt[32 * q : 32 * q + 32 : 16, :]
+                nc.sync.dma_start(compact[32 * q : 32 * q + 32, :, :], rows.rearrange("hh (blk b) -> blk hh b", b=32))
+            turned = keep.tile([P, 2, 32], F32, name="wgt_turned", align_bytes=64)
+            for hh in range(2):
+                nc.vector.transpose(turned[:, hh, :], compact[:, hh, :])
+            wgt_sb[0] = keep.tile([P, J], F32, name="wgt_all", align_bytes=64)
+            for h in range(HALVES):
+                spread = keep.tile([P, HALF], F32, name="wgt_spread_%d" % h, align_bytes=64)
+                src = turned[:, :, 16 * h : 16 * h + 16].rearrange("p hh blk -> p blk hh").unsqueeze(3).to_broadcast([P, 16, 2, 16])
+                (nc.vector.tensor_copy, nc.scalar.copy)[h](spread[:].rearrange("p (blk hh r) -> p blk hh r", hh=2, r=16), src)
+                nc.vector.transpose(wgt_sb[0][:, h * HALF : (h + 1) * HALF], spread[:])
 
         def wgt_cols(c0, c1):
             base = max(b for b in wgt_sb if b <= c0)
             return wgt_sb[base][:, c0 - base : c1 - base]
 
-        def LW(m, a, c):
+        def LW(m, a):
             w = (wk, wv)[m]
-            w_raw[m, a, c] = keep.tile([P, PACK, WCOLS], F32, name="w_raw_%d_%d_%d" % (m, a, c))
-            rows = w[a * K_PASS : (a + 1) * K_PASS, c * WCOLS : (c + 1) * WCOLS]
-            nc.sync.dma_start(w_raw[m, a, c][:], rows.rearrange("(p i) n -> p i n", i=PACK))
+            w_raw[m, a] = keep.tile([P, PACK, N], F32, name="w_raw_%d_%d" % (m, a))
+            nc.sync.dma_start(w_raw[m, a][:], w[a * K_PASS : (a + 1) * K_PASS, :].rearrange("(p i) n -> p i n", i=PACK))
 
-        def LS(n, h):
-            st_sb[n, h] = keep.tile([P, HALF], F32, name="st_%d_%d" % (n, h))
-            nc.sync.dma_start(st_sb[n, h][:], st[n * P : (n + 1) * P, h * HALF : (h + 1) * HALF])
+        def LS(n):
+            st_sb[n] = keep.tile([P, J], F32, name="st_%d" % n)
+            nc.sync.dma_start(st_sb[n][:], st[n * P : (n + 1) * P, :])
 
         def span(a, c):
             c0 = sum(CHUNKS[a][:c])
             return c0, c0 + CHUNKS[a][c]
 
-        def G(a, i, c):
-            c0, c1 = span(a, c)
-            if (a, c) not in picked:
-                picked[a, c] = keep.tile([P, PACK, c1 - c0], F32, name="picked_%d_%d" % (a, c))
+        def G(a, i, c0=0, c1=J):
+            if a not in picked:
+                picked[a] = keep.tile([P, PACK, J], F32, name="picked_%d" % a)
             nc.vector.tensor_tensor(
-                picked[a, c][:, i, :], planes[a, i][:].indirect(offsets[:, c0 // 16 : c1 // 16]), wgt_cols(c0, c1), MULT
+                picked[a][:, i, c0:c1], planes[a, i][:].indirect(offsets[:, c0 // 16 : c1 // 16]), wgt_sb[0][:, c0:c1], MULT
             )
 
         def IX(a, c, eng):
             c0, c1 = span(a, c)
-            xg[a, c] = ring.tile([P, c1 - c0, PACK], BF16, name="x_grouped", align_bytes=64, bufs=4)
-            interleave(eng, xg[a, c][:], picked[a, c][:])
+            xg[a, c] = ring.tile([P, c1 - c0, PACK], BF16, name="x_grouped", align_bytes=64, bufs=5)
+            interleave(eng, xg[a, c][:], picked[a][:, :, c0:c1])
 
         def QX(a, c):
             c0, c1 = span(a, c)
             h = c0 // HALF
             if (a, h) not in x_codes:
-                x_codes[a, h] = keep.tile([P, HALF], U32, name="x_codes_%d_%d" % (a, h), align_bytes=64)
+                x_codes[a, h] = keep.tile([P, HALF], U32, name="x_codes_%d_%d" % (a, h), tag=XT.get((a, h), "x_codes_%d_%d" % (a, h)), align_bytes=64)
                 x_scales[a, h] = keep.tile([P, HALF], U8, name="x_scales_%d_%d" % (a, h), align_bytes=64)
             cols = slice(c0 - h * HALF, c1 - h * HALF)
             quantize(x_codes[a, h][:, cols], x_scales[a, h][:, cols], xg[a, c][:])
 
         def IW(m, a, c, eng):
-            wg[m, a, c] = ring.tile([P, WCOLS, PACK], BF16, name="w_grouped", align_bytes=64, bufs=4)
-            interleave(eng, wg[m, a, c][:], w_raw[m, a, c][:])
+            wg[m, a, c] = ring.tile([P, WCOLS, PACK], BF16, name="w_grouped", align_bytes=64, bufs=6)
+            interleave(eng, wg[m, a, c][:], w_raw[m, a][:, :, c * WCOLS : (c + 1) * WCOLS])
 
         def QW(m, a, c):
-            w_codes[m, a, c] = keep.tile([P, WCOLS], U32, name="w_codes_%d_%d_%d" % (m, a, c), align_bytes=64)
-            w_scales[m, a, c] = keep.tile([P, WCOLS], U8, name="w_scales_%d_%d_%d" % (m, a, c), align_bytes=64)
-            quantize(w_codes[m, a, c][:], w_scales[m, a, c][:], wg[m, a, c][:])
+            if m not in w_codes:
+                w_codes[m] = keep.tile([P, PASSES, N], U32, name="w_codes_%d" % m, tag=WT.get(m, "w_codes_%d" % m), align_bytes=64)
+                w_scales[m] = keep.tile([P, PASSES, N], U8, name="w_scales_%d" % m, align_bytes=64)
+            cols = slice(c * WCOLS, (c + 1) * WCOLS)
+            quantize(w_codes[m][:, a, cols], w_scales[m][:, a, cols], wg[m, a, c][:])
 
         def MM(m, a, n, h):
             banks = (ke, ve)[m]
             if a == 0:
                 banks[n, h] = psum.tile([P, HALF], F32, name=("ke", "ve")[m], tag="bank_%d" % BANK(m, n, h))
-            c, r = divmod(n * P, WCOLS)
-            cols = slice(r, r + P)
+            cols = slice(n * P, (n + 1) * P)
             nc.tensor.matmul_mx(
                 out=banks[n, h][:],
-                lhsT=w_codes[m, a, c][:, cols].bitcast(FP8X4),
-                lhsT_scale=w_scales[m, a, c][:, cols],
+                lhsT=w_codes[m][:, a, cols].bitcast(FP8X4),
+                lhsT_scale=w_scales[m][:, a, cols],
                 rhs=x_codes[a, h][:].bitcast(FP8X4),
                 rhs_scale=x_scales[a, h][:],
                 start=(a == 0),
@@ -129,62 +140,74 @@ def tile_list_silu_kernel(tc, xT, wgt, wk, wv, st, offs, out):
 
         def A(n, h):
             f = ring.tile([P, HALF], F32, name="f", bufs=4)
-            nc.vector.tensor_tensor(f[:], ke[n, h][:], st_sb[n, h][:], MULT)
+            nc.vector.tensor_tensor(f[:], ke[n, h][:], st_sb[n][:, h * HALF : (h + 1) * HALF], MULT)
             gate[n, h] = keep.tile([P, HALF], F32, name="gate_%d_%d" % (n, h))
             nc.scalar.activation(gate[n, h][:], f[:], SILU)
 
         def C(n, h, eng="V"):
-            res = keep.tile([P, HALF], F32, name="res", tag="st_%d_%d" % (n, h))
+            if n not in res:
+                res[n] = keep.tile([P, J], F32, name="res_%d" % n, tag="plane_0_%d" % n, align_bytes=64)
+            dst = res[n][:, h * HALF : (h + 1) * HALF]
             if eng == "V":
-                nc.vector.tensor_tensor(res[:], ve[n, h][:], gate[n, h][:], MULT)
+                nc.vector.tensor_tensor(dst, ve[n, h][:], gate[n, h][:], MULT)
             else:
                 vs = ring.tile([P, HALF], F32, name="ve_sb", bufs=2)
                 nc.scalar.copy(vs[:], ve[n, h][:])
-                nc.gpsimd.tensor_tensor(res[:], vs[:], gate[n, h][:], MULT)
-            nc.sync.dma_start(out[n * P : (n + 1) * P, h * HALF : (h + 1) * HALF], res[:])
+                nc.gpsimd.tensor_tensor(dst, vs[:], gate[n, h][:], MULT)
+
+        def ST(n, c0=0, c1=J):
+            nc.sync.dma_start(out[n * P : (n + 1) * P, c0:c1], res[n][:, c0:c1])
 
         def BANK(m, n, h):
             return 2 * n + h
 
-        warm = keep.tile([P, 8], F32, name="warm")
-        nc.vector.memset(warm[:], 0.0)
-        nc.scalar.activation(warm[:, 0:1], warm[:, 1:2], SILU)
+        def WARM():
+            warm = keep.tile([P, 8], F32, name="warm")
+            nc.gpsimd.memset(warm[:], 0.0)
+            nc.scalar.activation(warm[:, 0:1], warm[:, 1:2], SILU)
 
-        LX(0, 0); LG(0, 512); LG(512, 1024); LX(0, 1); LX(0, 2); LX(0, 3); LX(1, 0); LW(0, 0, 0); LW(0, 0, 1); LX(1, 1); LW(0, 1, 0); LX(1, 2); LW(0, 1, 1); LX(1, 3); LW(1, 0, 0); LW(1, 1, 0)
-        for n in range(4):
-            LS(n, 0)
-        LW(1, 0, 1); LW(1, 1, 1)
-        for n in range(4):
-            LS(n, 1)
-        E1, E2, E3 = "VSS"
-        for i in range(4):
-            for c in range(len(CHUNKS[0])):
-                G(0, i, c)
-        for c in range(len(CHUNKS[0])):
-            IX(0, c, "S"); QX(0, c)
-        for a in range(2):
+        LG(); LX(0, 0); WARM()
+        nc.sync.dma_start(offsets[:], offs)
+        LX(0, 1); LX(0, 2); LX(0, 3); LX(1, 0); LX(1, 1); LW(0, 0); LX(1, 2); LW(0, 1); LW(1, 0); LX(1, 3); LW(1, 1); LS(0); LS(1); LS(2); LS(3)
+        GC = "VVVVVVVV"
+        def KE(n, h):
+            MM(0, 1, n, h); A(n, h)
+        def VE(n, h):
+            MM(1, 0, n, h); MM(1, 1, n, h); C(n, h, GC[2 * n + h])
+            if n >= 2:
+                ST(n, h * HALF, (h + 1) * HALF)
+            elif h == 1:
+                ST(n)
+        def W(m, a, eng="S", tag=None):
             for c in range(2):
-                IW(0, a, c, "S"); QW(0, a, c)
-        for h in range(2):
-            for n in range(4):
-                MM(0, 0, n, h)
-        IW(1, 0, 0, "S"); QW(1, 0, 0)
+                IW(m, a, c, eng); QW(m, a, c, tag if c else None)
         for i in range(4):
-            for c in range(len(CHUNKS[1])):
-                G(1, i, c)
+            G(0, i)
+        for c in range(2):
+            IX(0, c, "S"); QX(0, c)
+        for i in range(3):
+            G(1, i)
+        for m, a in ((0, 0), (0, 1)):
+            for c in range(2):
+                IW(m, a, c, "S"); QW(m, a, c)
+        IW(1, 0, 0, "S"); QW(1, 0, 0); IW(1, 0, 1, "S")
+        for n in range(4):
+            for h in range(2):
+                MM(0, 0, n, h)
+        for c in range(len(CHUNKS[1])):
+            G(1, 3, *span(1, c))
+
+        QW(1, 0, 1)
         for c in range(len(CHUNKS[1])):
             IX(1, c, "S"); QX(1, c)
-        for h in range(2):
-            for n in range(4):
-                MM(0, 1, n, h)
-        IW(1, 1, 0, E1); QW(1, 1, 0)
-        for n in range(4):
-            A(n, 0)
-        for n in range(2):
-            MM(1, 0, n, 0); MM(1, 1, n, 0); C(n, 0)
-        IW(1, 0, 1, E2); QW(1, 0, 1)
-        IW(1, 1, 1, E3); QW(1, 1, 1)
-        for n in range(4):
-            A(n, 1)
-        for n, h in ((0, 1), (1, 1), (2, 0), (3, 0), (2, 1), (3, 1)):
-            MM(1, 0, n, h); MM(1, 1, n, h); C(n, h)
+        IW(1, 1, 0, "S")
+        KE(0, 0); KE(1, 0); KE(2, 0); KE(0, 1)
+        QW(1, 1, 0)
+        KE(1, 1)
+        VE(0, 0); VE(0, 1)
+        IW(1, 1, 1, "S")
+        KE(3, 0)
+        VE(1, 0)
+        QW(1, 1, 1)
+        KE(2, 1); VE(1, 1); KE(3, 1)
+        VE(2, 0); VE(2, 1); VE(3, 0); VE(3, 1)

@@ -4,6 +4,7 @@ import concourse.mybir as mybir
 
 K, N, T, J = 1024, 512, 2048, 1024
 FLOPS = 2 * 2 * K * N * J
+BYTES = 4 * (K * T + 8 * J + 2 * K * N + 2 * N * J) + 2 * 8 * J
 
 F32 = mybir.dt.float32
 BF16 = mybir.dt.bfloat16
@@ -12,202 +13,203 @@ U16 = mybir.dt.uint16
 U8 = mybir.dt.uint8
 FP8X4 = mybir.dt.float8_e4m3fn_x4
 MULT = mybir.AluOpType.mult
-ADD = mybir.AluOpType.add
 SILU = mybir.ActivationFunctionType.Silu
 
 P = 128
 PACK = 4
 K_PASS = P * PACK
 PASSES = K // K_PASS
-HALF = 512
-HALVES = J // HALF
+LAST_PASS = PASSES - 1
+BANK = 512
+HALVES = J // BANK
 N_TILES = N // P
-CHUNKS = [[512,512],[256,256,256,256]]
-WCOLS = 256
-XT = {}
-WT = {0: "plane_1_2"}
+GROUP = 16
+SQUARE = 32
+KEYS, VALUES = 0, 1
+X_PIECE = 256
+X_PIECES = J // X_PIECE
+W_PIECE = 256
+W_PIECES = N // W_PIECE
+MX_ALIGN = 64
+
+
+def interleave(copy, grouped, rows):
+    copy(grouped.rearrange("p (c e) i -> p c i e", e=4), rows.rearrange("p i (c e) -> p c i e", e=4))
+
+
+def quantize(nc, codes, scales, grouped):
+    nc.vector.quantize_mx(out=codes.bitcast(FP8X4), scales=scales, in_=grouped.rearrange("p w i -> p (w i)"))
+
+
+def spread_wgt(nc, pool, wgt):
+    compact = pool.tile([P, 2, SQUARE], F32, name="wgt_compact", align_bytes=MX_ALIGN)
+    for q in range(P // SQUARE):
+        rows = wgt[SQUARE * q : SQUARE * (q + 1) : GROUP, :]
+        nc.sync.dma_start(compact[SQUARE * q : SQUARE * (q + 1), :, :], rows.rearrange("u (b e) -> b u e", e=SQUARE))
+    turned = pool.tile([P, 2, SQUARE], F32, name="wgt_turned", align_bytes=MX_ALIGN)
+    for u in range(2):
+        nc.vector.transpose(turned[:, u, :], compact[:, u, :])
+    full = pool.tile([P, J], F32, name="wgt_full", align_bytes=MX_ALIGN)
+    blocks = BANK // SQUARE
+    for h, copy in enumerate((nc.vector.tensor_copy, nc.scalar.copy)):
+        spread = pool.tile([P, BANK], F32, name="wgt_spread_%d" % h, align_bytes=MX_ALIGN)
+        values = turned[:, :, h * blocks : (h + 1) * blocks].rearrange("p u b -> p b u")
+        copy(
+            spread[:].rearrange("p (b u r) -> p b u r", u=2, r=GROUP),
+            values.unsqueeze(3).to_broadcast([P, blocks, 2, GROUP]),
+        )
+        nc.vector.transpose(full[:, h * BANK : (h + 1) * BANK], spread[:])
+    return full
 
 
 def tile_list_silu_kernel(tc, xT, wgt, wk, wv, st, offs, out):
     nc = tc.nc
     with ExitStack() as ctx:
         keep = ctx.enter_context(tc.tile_pool(name="keep", bufs=1))
-        ring = ctx.enter_context(tc.tile_pool(name="ring", bufs=3))
+        ring = ctx.enter_context(tc.tile_pool(name="ring", bufs=1))
         psum = ctx.enter_context(tc.psum_pool(name="psum", bufs=1))
 
-        offsets = keep.tile([P, J // 16], U16, name="offsets")
-
+        offsets = keep.tile([P, J // GROUP], U16, name="offsets")
         x_rows = xT.rearrange("(a p i) t -> a i p t", a=PASSES, i=PACK)
-        planes, w_raw, st_sb, wgt_sb = {}, {}, {}, {}
-        picked, x_codes, x_scales, w_codes, w_scales = {}, {}, {}, {}, {}
-        ke, ve, gate, xg, wg, res = {}, {}, {}, {}, {}, {}
+        planes, w_raw, st_rows = {}, {}, {}
 
-        def interleave(eng, grouped, rows):
-            dst = grouped.rearrange("p (c i) t -> p c t i", i=4)
-            src = rows.rearrange("p t (c i) -> p c t i", i=4)
-            if eng == "S":
-                nc.scalar.copy(dst, src)
-            elif eng == "V":
-                nc.vector.tensor_copy(dst, src)
-            else:
-                nc.gpsimd.tensor_scalar(dst, src, 1.0, 0.0, MULT, ADD)
-
-        def quantize(codes, scales, grouped):
-            nc.vector.quantize_mx(out=codes.bitcast(FP8X4), scales=scales, in_=grouped.rearrange("p w t -> p (w t)"))
-
-        def LX(a, i):
-            planes[a, i] = keep.tile([P, T], F32, name="plane_%d_%d" % (a, i), align_bytes=64)
+        def load_plane(a, i):
+            planes[a, i] = keep.tile([P, T], F32, name="plane_%d_%d" % (a, i), align_bytes=MX_ALIGN)
             nc.sync.dma_start(planes[a, i][:], x_rows[a, i])
 
-        def LG():
-            compact = keep.tile([P, 2, 32], F32, name="wgt_compact", align_bytes=64)
-            for q in range(4):
-                rows = wgt[32 * q : 32 * q + 32 : 16, :]
-                nc.sync.dma_start(compact[32 * q : 32 * q + 32, :, :], rows.rearrange("hh (blk b) -> blk hh b", b=32))
-            turned = keep.tile([P, 2, 32], F32, name="wgt_turned", align_bytes=64)
-            for hh in range(2):
-                nc.vector.transpose(turned[:, hh, :], compact[:, hh, :])
-            wgt_sb[0] = keep.tile([P, J], F32, name="wgt_all", align_bytes=64)
-            for h in range(HALVES):
-                spread = keep.tile([P, HALF], F32, name="wgt_spread_%d" % h, align_bytes=64)
-                src = turned[:, :, 16 * h : 16 * h + 16].rearrange("p hh blk -> p blk hh").unsqueeze(3).to_broadcast([P, 16, 2, 16])
-                (nc.vector.tensor_copy, nc.scalar.copy)[h](spread[:].rearrange("p (blk hh r) -> p blk hh r", hh=2, r=16), src)
-                nc.vector.transpose(wgt_sb[0][:, h * HALF : (h + 1) * HALF], spread[:])
-
-        def wgt_cols(c0, c1):
-            base = max(b for b in wgt_sb if b <= c0)
-            return wgt_sb[base][:, c0 - base : c1 - base]
-
-        def LW(m, a):
-            w = (wk, wv)[m]
+        def load_w(m, a):
+            rows = (wk, wv)[m][a * K_PASS : (a + 1) * K_PASS, :]
             w_raw[m, a] = keep.tile([P, PACK, N], F32, name="w_raw_%d_%d" % (m, a))
-            nc.sync.dma_start(w_raw[m, a][:], w[a * K_PASS : (a + 1) * K_PASS, :].rearrange("(p i) n -> p i n", i=PACK))
+            nc.sync.dma_start(w_raw[m, a][:], rows.rearrange("(p i) n -> p i n", i=PACK))
 
-        def LS(n):
-            st_sb[n] = keep.tile([P, J], F32, name="st_%d" % n)
-            nc.sync.dma_start(st_sb[n][:], st[n * P : (n + 1) * P, :])
+        def load_st(n):
+            st_rows[n] = keep.tile([P, J], F32, name="st_%d" % n)
+            nc.sync.dma_start(st_rows[n][:], st[n * P : (n + 1) * P, :])
 
-        def span(a, c):
-            c0 = sum(CHUNKS[a][:c])
-            return c0, c0 + CHUNKS[a][c]
+        wgt_full = spread_wgt(nc, keep, wgt)
+        load_plane(0, 0)
+        warm = keep.tile([P, 8], F32, name="warm")
+        nc.gpsimd.memset(warm[:], 0.0)
+        nc.scalar.activation(warm[:, 0:1], warm[:, 1:2], SILU)
+        nc.sync.dma_start(offsets[:], offs)
+        for a, i in [divmod(plane, PACK) for plane in range(1, PASSES * PACK - 1)]:
+            load_plane(a, i)
+        load_w(KEYS, 0)
+        load_plane(LAST_PASS, PACK - 1)
+        load_w(KEYS, LAST_PASS)
+        load_st(0)
+        for a in range(PASSES):
+            load_w(VALUES, a)
+        for n in range(1, N_TILES):
+            load_st(n)
 
-        def G(a, i, c0=0, c1=J):
-            if a not in picked:
-                picked[a] = keep.tile([P, PACK, J], F32, name="picked_%d" % a)
-            nc.vector.tensor_tensor(
-                picked[a][:, i, c0:c1], planes[a, i][:].indirect(offsets[:, c0 // 16 : c1 // 16]), wgt_sb[0][:, c0:c1], MULT
-            )
+        picked = [keep.tile([P, PACK, J], F32, name="picked_%d" % a) for a in range(PASSES)]
+        x_grouped, x_codes, x_scales = {}, {}, {}
+        w_grouped, w_codes, w_scales = {}, {}, {}
+        ke, ve, gates, results = {}, {}, {}, {}
 
-        def IX(a, c, eng):
-            c0, c1 = span(a, c)
-            xg[a, c] = ring.tile([P, c1 - c0, PACK], BF16, name="x_grouped", align_bytes=64, bufs=5)
-            interleave(eng, xg[a, c][:], picked[a][:, :, c0:c1])
+        def gather(a, i, j0, j1):
+            window = planes[a, i][:].indirect(offsets[:, j0 // GROUP : j1 // GROUP])
+            nc.vector.tensor_tensor(picked[a][:, i, j0:j1], window, wgt_full[:, j0:j1], MULT)
 
-        def QX(a, c):
-            c0, c1 = span(a, c)
-            h = c0 // HALF
+        def round_x(copy, a, j0, j1):
+            name = "x_grouped_%d_%d" % (a, j0)
+            x_grouped[a, j0] = keep.tile([P, j1 - j0, PACK], BF16, name=name, align_bytes=MX_ALIGN)
+            interleave(copy, x_grouped[a, j0][:], picked[a][:, :, j0:j1])
+
+        def quantize_x(a, j0, j1):
+            h = j0 // BANK
             if (a, h) not in x_codes:
-                x_codes[a, h] = keep.tile([P, HALF], U32, name="x_codes_%d_%d" % (a, h), tag=XT.get((a, h), "x_codes_%d_%d" % (a, h)), align_bytes=64)
-                x_scales[a, h] = keep.tile([P, HALF], U8, name="x_scales_%d_%d" % (a, h), align_bytes=64)
-            cols = slice(c0 - h * HALF, c1 - h * HALF)
-            quantize(x_codes[a, h][:, cols], x_scales[a, h][:, cols], xg[a, c][:])
+                x_codes[a, h] = keep.tile([P, BANK], U32, name="x_codes_%d_%d" % (a, h), align_bytes=MX_ALIGN)
+                x_scales[a, h] = keep.tile([P, BANK], U8, name="x_scales_%d_%d" % (a, h), align_bytes=MX_ALIGN)
+            cols = slice(j0 - h * BANK, j1 - h * BANK)
+            quantize(nc, x_codes[a, h][:, cols], x_scales[a, h][:, cols], x_grouped[a, j0][:])
 
-        def IW(m, a, c, eng):
-            wg[m, a, c] = ring.tile([P, WCOLS, PACK], BF16, name="w_grouped", align_bytes=64, bufs=6)
-            interleave(eng, wg[m, a, c][:], w_raw[m, a][:, :, c * WCOLS : (c + 1) * WCOLS])
+        def round_w(copy, m, a, c):
+            w_grouped[m, a, c] = ring.tile([P, W_PIECE, PACK], BF16, name="w_grouped", align_bytes=MX_ALIGN, bufs=6)
+            interleave(copy, w_grouped[m, a, c][:], w_raw[m, a][:, :, c * W_PIECE : (c + 1) * W_PIECE])
 
-        def QW(m, a, c):
+        def quantize_w(m, a, c):
             if m not in w_codes:
-                w_codes[m] = keep.tile([P, PASSES, N], U32, name="w_codes_%d" % m, tag=WT.get(m, "w_codes_%d" % m), align_bytes=64)
-                w_scales[m] = keep.tile([P, PASSES, N], U8, name="w_scales_%d" % m, align_bytes=64)
-            cols = slice(c * WCOLS, (c + 1) * WCOLS)
-            quantize(w_codes[m][:, a, cols], w_scales[m][:, a, cols], wg[m, a, c][:])
+                w_codes[m] = keep.tile([P, PASSES, N], U32, name="w_codes_%d" % m, align_bytes=MX_ALIGN)
+                w_scales[m] = keep.tile([P, PASSES, N], U8, name="w_scales_%d" % m, align_bytes=MX_ALIGN)
+            cols = slice(c * W_PIECE, (c + 1) * W_PIECE)
+            quantize(nc, w_codes[m][:, a, cols], w_scales[m][:, a, cols], w_grouped[m, a, c][:])
 
-        def MM(m, a, n, h):
-            banks = (ke, ve)[m]
+        def mx_pass(sums, m, a, n, h):
             if a == 0:
-                banks[n, h] = psum.tile([P, HALF], F32, name=("ke", "ve")[m], tag="bank_%d" % BANK(m, n, h))
+                sums[n, h] = psum.tile([P, BANK], F32, name="sums", tag="bank_%d" % (HALVES * n + h))
             cols = slice(n * P, (n + 1) * P)
             nc.tensor.matmul_mx(
-                out=banks[n, h][:],
+                out=sums[n, h][:],
                 lhsT=w_codes[m][:, a, cols].bitcast(FP8X4),
                 lhsT_scale=w_scales[m][:, a, cols],
                 rhs=x_codes[a, h][:].bitcast(FP8X4),
                 rhs_scale=x_scales[a, h][:],
                 start=(a == 0),
-                stop=(a == PASSES - 1),
+                stop=(a == LAST_PASS),
             )
 
-        def A(n, h):
-            f = ring.tile([P, HALF], F32, name="f", bufs=4)
-            nc.vector.tensor_tensor(f[:], ke[n, h][:], st_sb[n][:, h * HALF : (h + 1) * HALF], MULT)
-            gate[n, h] = keep.tile([P, HALF], F32, name="gate_%d_%d" % (n, h))
-            nc.scalar.activation(gate[n, h][:], f[:], SILU)
+        def gate_view(n, h):
+            return gates[n // 2][:, HALVES * (n % 2) + h, :]
 
-        def C(n, h, eng="V"):
-            if n not in res:
-                res[n] = keep.tile([P, J], F32, name="res_%d" % n, tag="plane_0_%d" % n, align_bytes=64)
-            dst = res[n][:, h * HALF : (h + 1) * HALF]
-            if eng == "V":
-                nc.vector.tensor_tensor(dst, ve[n, h][:], gate[n, h][:], MULT)
-            else:
-                vs = ring.tile([P, HALF], F32, name="ve_sb", bufs=2)
-                nc.scalar.copy(vs[:], ve[n, h][:])
-                nc.gpsimd.tensor_tensor(dst, vs[:], gate[n, h][:], MULT)
+        def make_gate(n, h):
+            mx_pass(ke, KEYS, LAST_PASS, n, h)
+            product = ring.tile([P, BANK], F32, name="product", bufs=N_TILES * HALVES)
+            nc.vector.tensor_tensor(product[:], ke[n, h][:], st_rows[n][:, h * BANK : (h + 1) * BANK], MULT)
+            if n // 2 not in gates:
+                tag = "w_raw_%d_%d" % (VALUES, n // 2)
+                gates[n // 2] = keep.tile([P, 2 * HALVES, BANK], F32, name="gates", tag=tag)
+            nc.scalar.activation(gate_view(n, h), product[:], SILU)
 
-        def ST(n, c0=0, c1=J):
-            nc.sync.dma_start(out[n * P : (n + 1) * P, c0:c1], res[n][:, c0:c1])
+        def make_result(n, h):
+            for a in range(PASSES):
+                mx_pass(ve, VALUES, a, n, h)
+            if n not in results:
+                results[n] = keep.tile([P, J], F32, name="result", tag="plane_0_%d" % n, align_bytes=MX_ALIGN)
+            cols = slice(h * BANK, (h + 1) * BANK)
+            nc.vector.tensor_tensor(results[n][:, cols], ve[n, h][:], gate_view(n, h), MULT)
+            nc.sync.dma_start(out[n * P : (n + 1) * P, cols], results[n][:, cols])
 
-        def BANK(m, n, h):
-            return 2 * n + h
+        for i in range(PACK):
+            gather(0, i, 0, J)
+        for h in range(HALVES):
+            round_x(nc.scalar.copy, 0, h * BANK, (h + 1) * BANK)
+            quantize_x(0, h * BANK, (h + 1) * BANK)
+        for i in range(PACK - 1):
+            gather(LAST_PASS, i, 0, J)
 
-        def WARM():
-            warm = keep.tile([P, 8], F32, name="warm")
-            nc.gpsimd.memset(warm[:], 0.0)
-            nc.scalar.activation(warm[:, 0:1], warm[:, 1:2], SILU)
+        for c in range(W_PIECES):
+            round_w(nc.scalar.copy, KEYS, 0, c)
+            quantize_w(KEYS, 0, c)
+        for n in range(N_TILES):
+            for h in range(HALVES):
+                mx_pass(ke, KEYS, 0, n, h)
 
-        LG(); LX(0, 0); WARM()
-        nc.sync.dma_start(offsets[:], offs)
-        LX(0, 1); LX(0, 2); LX(0, 3); LX(1, 0); LX(1, 1); LW(0, 0); LX(1, 2); LW(0, 1); LW(1, 0); LX(1, 3); LW(1, 1); LS(0); LS(1); LS(2); LS(3)
-        GC = "VVVVVVVV"
-        def KE(n, h):
-            MM(0, 1, n, h); A(n, h)
-        def VE(n, h):
-            MM(1, 0, n, h); MM(1, 1, n, h); C(n, h, GC[2 * n + h])
-            if n >= 2:
-                ST(n, h * HALF, (h + 1) * HALF)
-            elif h == 1:
-                ST(n)
-        def W(m, a, eng="S", tag=None):
-            for c in range(2):
-                IW(m, a, c, eng); QW(m, a, c, tag if c else None)
-        for i in range(4):
-            G(0, i)
-        for c in range(2):
-            IX(0, c, "S"); QX(0, c)
-        for i in range(3):
-            G(1, i)
-        for m, a in ((0, 0), (0, 1)):
-            for c in range(2):
-                IW(m, a, c, "S"); QW(m, a, c)
-        IW(1, 0, 0, "S"); QW(1, 0, 0); IW(1, 0, 1, "S")
-        for n in range(4):
-            for h in range(2):
-                MM(0, 0, n, h)
-        for c in range(len(CHUNKS[1])):
-            G(1, 3, *span(1, c))
+        spans = [(c * X_PIECE, (c + 1) * X_PIECE) for c in range(X_PIECES)]
+        first_half, second_half = spans[: X_PIECES // HALVES], spans[X_PIECES // HALVES :]
+        for j0, j1 in spans:
+            gather(LAST_PASS, PACK - 1, j0, j1)
+        for j0, j1 in first_half:
+            round_x(nc.scalar.copy, LAST_PASS, j0, j1)
+        round_w(nc.vector.tensor_copy, KEYS, LAST_PASS, 0)
+        for copy, (j0, j1) in zip((nc.scalar.copy, nc.vector.tensor_copy), second_half):
+            round_x(copy, LAST_PASS, j0, j1)
+        for j0, j1 in first_half:
+            quantize_x(LAST_PASS, j0, j1)
+        quantize_w(KEYS, LAST_PASS, 0)
+        for j0, j1 in second_half:
+            quantize_x(LAST_PASS, j0, j1)
 
-        QW(1, 0, 1)
-        for c in range(len(CHUNKS[1])):
-            IX(1, c, "S"); QX(1, c)
-        IW(1, 1, 0, "S")
-        KE(0, 0); KE(1, 0); KE(2, 0); KE(0, 1)
-        QW(1, 1, 0)
-        KE(1, 1)
-        VE(0, 0); VE(0, 1)
-        IW(1, 1, 1, "S")
-        KE(3, 0)
-        VE(1, 0)
-        QW(1, 1, 1)
-        KE(2, 1); VE(1, 1); KE(3, 1)
-        VE(2, 0); VE(2, 1); VE(3, 0); VE(3, 1)
+        later = [(KEYS, LAST_PASS, 1)] + [(VALUES, a, c) for a in range(PASSES) for c in range(W_PIECES)]
+        for m, a, c in later:
+            round_w(nc.scalar.copy, m, a, c)
+            quantize_w(m, a, c)
+
+        for step in range(N_TILES + 1):
+            if step < N_TILES:
+                for h in range(HALVES):
+                    make_gate(step, h)
+            if step > 0:
+                for h in range(HALVES):
+                    make_result(step - 1, h)

from contextlib import ExitStack

import concourse.mybir as mybir

K, N, T, J = 1024, 512, 2048, 1024
FLOPS = 2 * 2 * K * N * J
BYTES = 4 * (K * T + 8 * J + 2 * K * N + 2 * N * J) + 2 * 8 * J

F32 = mybir.dt.float32
BF16 = mybir.dt.bfloat16
U32 = mybir.dt.uint32
U16 = mybir.dt.uint16
U8 = mybir.dt.uint8
FP8X4 = mybir.dt.float8_e4m3fn_x4
MULT = mybir.AluOpType.mult
SILU = mybir.ActivationFunctionType.Silu

P = 128
PACK = 4
K_PASS = P * PACK
PASSES = K // K_PASS
LAST_PASS = PASSES - 1
BANK = 512
HALVES = J // BANK
N_TILES = N // P
GROUP = 16
SQUARE = 32
KEYS, VALUES = 0, 1
X_PIECE = 256
X_PIECES = J // X_PIECE
W_PIECE = 256
W_PIECES = N // W_PIECE
MX_ALIGN = 64


def interleave(copy, grouped, rows):
    copy(grouped.rearrange("p (c e) i -> p c i e", e=4), rows.rearrange("p i (c e) -> p c i e", e=4))


def quantize(nc, codes, scales, grouped):
    nc.vector.quantize_mx(out=codes.bitcast(FP8X4), scales=scales, in_=grouped.rearrange("p w i -> p (w i)"))


def spread_wgt(nc, pool, wgt):
    compact = pool.tile([P, 2, SQUARE], F32, name="wgt_compact", align_bytes=MX_ALIGN)
    for q in range(P // SQUARE):
        rows = wgt[SQUARE * q : SQUARE * (q + 1) : GROUP, :]
        nc.sync.dma_start(compact[SQUARE * q : SQUARE * (q + 1), :, :], rows.rearrange("u (b e) -> b u e", e=SQUARE))
    turned = pool.tile([P, 2, SQUARE], F32, name="wgt_turned", align_bytes=MX_ALIGN)
    for u in range(2):
        nc.vector.transpose(turned[:, u, :], compact[:, u, :])
    full = pool.tile([P, J], F32, name="wgt_full", align_bytes=MX_ALIGN)
    blocks = BANK // SQUARE
    for h, copy in enumerate((nc.vector.tensor_copy, nc.scalar.copy)):
        spread = pool.tile([P, BANK], F32, name="wgt_spread_%d" % h, align_bytes=MX_ALIGN)
        values = turned[:, :, h * blocks : (h + 1) * blocks].rearrange("p u b -> p b u")
        copy(
            spread[:].rearrange("p (b u r) -> p b u r", u=2, r=GROUP),
            values.unsqueeze(3).to_broadcast([P, blocks, 2, GROUP]),
        )
        nc.vector.transpose(full[:, h * BANK : (h + 1) * BANK], spread[:])
    return full


def tile_list_silu_kernel(tc, xT, wgt, wk, wv, st, offs, out):
    nc = tc.nc
    with ExitStack() as ctx:
        keep = ctx.enter_context(tc.tile_pool(name="keep", bufs=1))
        ring = ctx.enter_context(tc.tile_pool(name="ring", bufs=1))
        psum = ctx.enter_context(tc.psum_pool(name="psum", bufs=1))

        offsets = keep.tile([P, J // GROUP], U16, name="offsets")
        x_rows = xT.rearrange("(a p i) t -> a i p t", a=PASSES, i=PACK)
        planes, w_raw, st_rows = {}, {}, {}

        def load_plane(a, i):
            planes[a, i] = keep.tile([P, T], F32, name="plane_%d_%d" % (a, i), align_bytes=MX_ALIGN)
            nc.sync.dma_start(planes[a, i][:], x_rows[a, i])

        def load_w(m, a):
            rows = (wk, wv)[m][a * K_PASS : (a + 1) * K_PASS, :]
            w_raw[m, a] = keep.tile([P, PACK, N], F32, name="w_raw_%d_%d" % (m, a))
            nc.sync.dma_start(w_raw[m, a][:], rows.rearrange("(p i) n -> p i n", i=PACK))

        def load_st(n):
            st_rows[n] = keep.tile([P, J], F32, name="st_%d" % n)
            nc.sync.dma_start(st_rows[n][:], st[n * P : (n + 1) * P, :])

        wgt_full = spread_wgt(nc, keep, wgt)
        load_plane(0, 0)
        warm = keep.tile([P, 8], F32, name="warm")
        nc.gpsimd.memset(warm[:], 0.0)
        nc.scalar.activation(warm[:, 0:1], warm[:, 1:2], SILU)
        nc.sync.dma_start(offsets[:], offs)
        for a, i in [divmod(plane, PACK) for plane in range(1, PASSES * PACK - 1)]:
            load_plane(a, i)
        load_w(KEYS, 0)
        load_plane(LAST_PASS, PACK - 1)
        load_w(KEYS, LAST_PASS)
        load_st(0)
        for a in range(PASSES):
            load_w(VALUES, a)
        for n in range(1, N_TILES):
            load_st(n)

        picked = [keep.tile([P, PACK, J], F32, name="picked_%d" % a) for a in range(PASSES)]
        x_grouped, x_codes, x_scales = {}, {}, {}
        w_grouped, w_codes, w_scales = {}, {}, {}
        ke, ve, gates, results = {}, {}, {}, {}

        def gather(a, i, j0, j1):
            window = planes[a, i][:].indirect(offsets[:, j0 // GROUP : j1 // GROUP])
            nc.vector.tensor_tensor(picked[a][:, i, j0:j1], window, wgt_full[:, j0:j1], MULT)

        def round_x(copy, a, j0, j1):
            name = "x_grouped_%d_%d" % (a, j0)
            x_grouped[a, j0] = keep.tile([P, j1 - j0, PACK], BF16, name=name, align_bytes=MX_ALIGN)
            interleave(copy, x_grouped[a, j0][:], picked[a][:, :, j0:j1])

        def quantize_x(a, j0, j1):
            h = j0 // BANK
            if (a, h) not in x_codes:
                x_codes[a, h] = keep.tile([P, BANK], U32, name="x_codes_%d_%d" % (a, h), align_bytes=MX_ALIGN)
                x_scales[a, h] = keep.tile([P, BANK], U8, name="x_scales_%d_%d" % (a, h), align_bytes=MX_ALIGN)
            cols = slice(j0 - h * BANK, j1 - h * BANK)
            quantize(nc, x_codes[a, h][:, cols], x_scales[a, h][:, cols], x_grouped[a, j0][:])

        def round_w(copy, m, a, c):
            w_grouped[m, a, c] = ring.tile([P, W_PIECE, PACK], BF16, name="w_grouped", align_bytes=MX_ALIGN, bufs=6)
            interleave(copy, w_grouped[m, a, c][:], w_raw[m, a][:, :, c * W_PIECE : (c + 1) * W_PIECE])

        def quantize_w(m, a, c):
            if m not in w_codes:
                w_codes[m] = keep.tile([P, PASSES, N], U32, name="w_codes_%d" % m, align_bytes=MX_ALIGN)
                w_scales[m] = keep.tile([P, PASSES, N], U8, name="w_scales_%d" % m, align_bytes=MX_ALIGN)
            cols = slice(c * W_PIECE, (c + 1) * W_PIECE)
            quantize(nc, w_codes[m][:, a, cols], w_scales[m][:, a, cols], w_grouped[m, a, c][:])

        def mx_pass(sums, m, a, n, h):
            if a == 0:
                sums[n, h] = psum.tile([P, BANK], F32, name="sums", tag="bank_%d" % (HALVES * n + h))
            cols = slice(n * P, (n + 1) * P)
            nc.tensor.matmul_mx(
                out=sums[n, h][:],
                lhsT=w_codes[m][:, a, cols].bitcast(FP8X4),
                lhsT_scale=w_scales[m][:, a, cols],
                rhs=x_codes[a, h][:].bitcast(FP8X4),
                rhs_scale=x_scales[a, h][:],
                start=(a == 0),
                stop=(a == LAST_PASS),
            )

        def gate_view(n, h):
            return gates[n // 2][:, HALVES * (n % 2) + h, :]

        def make_gate(n, h):
            mx_pass(ke, KEYS, LAST_PASS, n, h)
            product = ring.tile([P, BANK], F32, name="product", bufs=N_TILES * HALVES)
            nc.vector.tensor_tensor(product[:], ke[n, h][:], st_rows[n][:, h * BANK : (h + 1) * BANK], MULT)
            if n // 2 not in gates:
                tag = "w_raw_%d_%d" % (VALUES, n // 2)
                gates[n // 2] = keep.tile([P, 2 * HALVES, BANK], F32, name="gates", tag=tag)
            nc.scalar.activation(gate_view(n, h), product[:], SILU)

        def make_result(n, h):
            for a in range(PASSES):
                mx_pass(ve, VALUES, a, n, h)
            if n not in results:
                results[n] = keep.tile([P, J], F32, name="result", tag="plane_0_%d" % n, align_bytes=MX_ALIGN)
            cols = slice(h * BANK, (h + 1) * BANK)
            nc.vector.tensor_tensor(results[n][:, cols], ve[n, h][:], gate_view(n, h), MULT)
            nc.sync.dma_start(out[n * P : (n + 1) * P, cols], results[n][:, cols])

        for i in range(PACK):
            gather(0, i, 0, J)
        for h in range(HALVES):
            round_x(nc.scalar.copy, 0, h * BANK, (h + 1) * BANK)
            quantize_x(0, h * BANK, (h + 1) * BANK)
        for i in range(PACK - 1):
            gather(LAST_PASS, i, 0, J)

        for c in range(W_PIECES):
            round_w(nc.scalar.copy, KEYS, 0, c)
            quantize_w(KEYS, 0, c)
        for n in range(N_TILES):
            for h in range(HALVES):
                mx_pass(ke, KEYS, 0, n, h)

        spans = [(c * X_PIECE, (c + 1) * X_PIECE) for c in range(X_PIECES)]
        first_half, second_half = spans[: X_PIECES // HALVES], spans[X_PIECES // HALVES :]
        for j0, j1 in spans:
            gather(LAST_PASS, PACK - 1, j0, j1)
        for j0, j1 in first_half:
            round_x(nc.scalar.copy, LAST_PASS, j0, j1)
        round_w(nc.vector.tensor_copy, KEYS, LAST_PASS, 0)
        for copy, (j0, j1) in zip((nc.scalar.copy, nc.vector.tensor_copy), second_half):
            round_x(copy, LAST_PASS, j0, j1)
        for j0, j1 in first_half:
            quantize_x(LAST_PASS, j0, j1)
        quantize_w(KEYS, LAST_PASS, 0)
        for j0, j1 in second_half:
            quantize_x(LAST_PASS, j0, j1)

        later = [(KEYS, LAST_PASS, 1)] + [(VALUES, a, c) for a in range(PASSES) for c in range(W_PIECES)]
        for m, a, c in later:
            round_w(nc.scalar.copy, m, a, c)
            quantize_w(m, a, c)

        for step in range(N_TILES + 1):
            if step < N_TILES:
                for h in range(HALVES):
                    make_gate(step, h)
            if step > 0:
                for h in range(HALVES):
                    make_result(step - 1, h)
